import numpy as np
CORES = [5,13,21,29,37,45,53,61,197,205,213,221,229,237,245,253]
N = 16
def setup_inputs(rng):
    return {"x1": rng.standard_normal((N, 128, 256), dtype=np.float32), "x2": rng.standard_normal((N, 128, 1), dtype=np.float32), "x3": rng.standard_normal((N, 128, 1024), dtype=np.float32), "x4": rng.standard_normal((N, 128, 64), dtype=np.float32)}
def reference(x1, x2, x3, x4):
    out = {}
    s = x1.sum(axis=0, dtype=np.float64).astype(x1.dtype)
    out["y1"] = np.broadcast_to(s, (N,) + s.shape)
    s = x2.sum(axis=0, dtype=np.float64).astype(x2.dtype)
    out["y2"] = np.broadcast_to(s, (N,) + s.shape)
    s = x3.sum(axis=0, dtype=np.float64).astype(x3.dtype)
    out["y3"] = np.broadcast_to(s, (N,) + s.shape)
    s = x4.sum(axis=0, dtype=np.float64).astype(x4.dtype)
    out["y4"] = np.broadcast_to(s, (N,) + s.shape)
    return out

@@ -1,0 +1,85 @@
+from concourse.bass import DstId, RemoteDMATransfer
+
+NA, NB = 168, 176
+HELPER = 2
+OFF = 0x00FF
+ON = 0xFF00
+
+SCRATCH = {
+    "a": ("dram", [9, 128, NA], "float32"),
+    "b": ("dram", [9, 128, NB], "float32"),
+}
+SEMAPHORES = ["loaded", "sent", "landed", "mate", "arrived", "stored"]
+
+
+def places(T, pre):
+    t1, t2, t3, t4 = T[pre + "1"], T[pre + "2"], T[pre + "3"], T[pre + "4"]
+    return [
+        (T.a[0:6], t3[0:126, :]),
+        (T.a[6], t1[0:84, :]),
+        (T.b[0, 0:64, :], t1[84:128, :]),
+        (T.b[0, 64:96, :], t4[0:88, :]),
+        (T.b[0, 96:112, 0:160], t4[88:128, :]),
+        (T.b[0, 112:128, 0:128], t3[126:128, :]),
+        (T.b[0, 96:104, 160:176], t2[:, :]),
+    ]
+
+
+def padding(T):
+    return [
+        (T.b[0, 104:112, 160:176], T.x2[:, :]),
+        (T.b[0, 112:128, 128:176], T.x1[0:3, :]),
+    ]
+
+
+def rank_program(g, core, T, topo):
+    chip_base = core - core % 8
+    rank = T.rank_of(chip_base + 5)
+    if rank is None or core % 8 not in (5, HELPER):
+        return
+    pair, par = rank // 2, rank % 2
+    S = T.sem
+
+    def piece(k, slot):
+        return T.a[slot] if k < 7 else T.b[slot]
+
+    def bucket(k):
+        return T.a[k] if k < 7 else T.b[0]
+
+    if core % 8 == 5:
+        qs = [g.sync, g.scalar]
+        pl = places(T, "x") + padding(T)
+        for i, (buf, x) in enumerate(pl):
+            qs[i % 2].dma_start(buf, x).then_inc(S.loaded, 16)
+        g.wait_ge(S.loaded, 16 * len(pl))
+        for d in range(1, 9):
+            k = (pair + d) % 8
+            dst = T.cores[2 * k + par] - 5 + HELPER
+            rid, pid = topo.addr(dst, core)
+            g.remote_dma(piece(k, pair), bucket(k), S.landed, S.sent, pid, rid, ON if k == pair else OFF)
+        pl = places(T, "y")
+        for q in qs:
+            q.wait_ge(S.arrived, 8 * 8)
+        for i, (buf, y) in enumerate(pl):
+            qs[i % 2].dma_start(y, buf).then_inc(S.stored, 16)
+        g.wait_ge(S.sent, 8 * 8)
+        g.wait_ge(S.arrived, 8 * 8)
+        g.wait_ge(S.stored, 16 * len(pl))
+        return
+
+    k = pair
+    g.wait_ge(S.landed, 8 * 8)
+    mate = T.cores[rank ^ 1] - 5 + HELPER
+    rid, pid = topo.addr(mate, core)
+    g.remote_dma_fused([RemoteDMATransfer(
+        dst_ids=[DstId(rid=rid, pnc=pid)], dma_engine_mask=OFF, remote_sem=S.mate,
+        srcs=[piece(k, s) for s in range(8)], dsts=[piece(k, 8)], alu_op=1)], local_sem=S.sent)
+    g.wait_ge(S.mate, 8)
+    ids = []
+    for q in range(8):
+        rid, pid = topo.addr(T.cores[2 * q + par], core)
+        ids.append(DstId(rid=rid, pnc=pid))
+    g.remote_dma_fused([RemoteDMATransfer(
+        dst_ids=ids, dma_engine_mask=OFF, remote_sem=S.arrived,
+        srcs=[piece(k, s) for s in range(9)], dsts=[bucket(k) for q in range(8)], alu_op=1)], local_sem=S.sent)
+    g.wait_ge(S.sent, 16)

@@ -1,85 +1,98 @@
 from concourse.bass import DstId, RemoteDMATransfer
 
-NA, NB = 168, 176
-HELPER = 2
+WU, WV = 64, 42
+HELPER = (2, 3, 2)
 OFF = 0x00FF
 ON = 0xFF00
 
 SCRATCH = {
-    "a": ("dram", [9, 128, NA], "float32"),
-    "b": ("dram", [9, 128, NB], "float32"),
+    "u": ("dram", [16, 128, WU], "float32"),
+    "v": ("dram", [9 * 128, WV], "float32"),
 }
-SEMAPHORES = ["loaded", "sent", "landed", "mate", "arrived", "stored"]
+SEMAPHORES = ["ld0", "ld1", "ld2", "land0", "land1", "land2", "mate0", "mate1", "mate2", "arr0", "arr1", "arr2",
+              "sent", "stored"]
 
 
 def places(T, pre):
     t1, t2, t3, t4 = T[pre + "1"], T[pre + "2"], T[pre + "3"], T[pre + "4"]
     return [
-        (T.a[0:6], t3[0:126, :]),
-        (T.a[6], t1[0:84, :]),
-        (T.b[0, 0:64, :], t1[84:128, :]),
-        (T.b[0, 64:96, :], t4[0:88, :]),
-        (T.b[0, 96:112, 0:160], t4[88:128, :]),
-        (T.b[0, 112:128, 0:128], t3[126:128, :]),
-        (T.b[0, 96:104, 160:176], t2[:, :]),
+        [(T.u[0:8], t3[0:64, :])],
+        [(T.u[8:16], t3[64:128, :])],
+        [(T.v[0:768, :], t1[0:126, :]),
+         (T.v[768:960, :], t4[0:126, :]),
+         (T.v[960:976, 0:32], t1[126:128, :]),
+         (T.v[976:980, 0:32], t4[126:128, :]),
+         (T.v[980:984, 0:32], t2[:, :])],
     ]
 
 
 def padding(T):
     return [
-        (T.b[0, 104:112, 160:176], T.x2[:, :]),
-        (T.b[0, 112:128, 128:176], T.x1[0:3, :]),
+        (T.v[960:984, 32:42], T.x1[0, 0:240]),
+        (T.v[984:1024, :], T.x3[0:2, 0:840]),
     ]
 
 
 def rank_program(g, core, T, topo):
-    chip_base = core - core % 8
-    rank = T.rank_of(chip_base + 5)
-    if rank is None or core % 8 not in (5, HELPER):
+    me = core % 8
+    rank = T.rank_of(core - me + 5)
+    if rank is None or (me != 5 and me not in HELPER):
         return
     pair, par = rank // 2, rank % 2
     S = T.sem
 
-    def piece(k, slot):
-        return T.a[slot] if k < 7 else T.b[slot]
+    def slot(c, s):
+        return T.u[s] if c < 2 else T.v[128 * s:128 * (s + 1), :]
 
-    def bucket(k):
-        return T.a[k] if k < 7 else T.b[0]
+    def bucket(c, k):
+        return T.u[8 * c + k] if c < 2 else T.v[128 * k:128 * (k + 1), :]
 
-    if core % 8 == 5:
-        qs = [g.sync, g.scalar]
-        pl = places(T, "x") + padding(T)
-        for i, (buf, x) in enumerate(pl):
-            qs[i % 2].dma_start(buf, x).then_inc(S.loaded, 16)
-        g.wait_ge(S.loaded, 16 * len(pl))
-        for d in range(1, 9):
-            k = (pair + d) % 8
-            dst = T.cores[2 * k + par] - 5 + HELPER
-            rid, pid = topo.addr(dst, core)
-            g.remote_dma(piece(k, pair), bucket(k), S.landed, S.sent, pid, rid, ON if k == pair else OFF)
-        pl = places(T, "y")
-        for q in qs:
-            q.wait_ge(S.arrived, 8 * 8)
-        for i, (buf, y) in enumerate(pl):
-            qs[i % 2].dma_start(y, buf).then_inc(S.stored, 16)
-        g.wait_ge(S.sent, 8 * 8)
-        g.wait_ge(S.arrived, 8 * 8)
-        g.wait_ge(S.stored, 16 * len(pl))
+    def dst_id(d):
+        rid, pid = topo.addr(d, core)
+        return DstId(rid=rid, pnc=pid)
+
+    if me == 5:
+        loads = places(T, "x")
+        loads[2] = loads[2] + padding(T)
+        stores = places(T, "y")
+        g.sync.dma_start(*loads[0][0]).then_inc(S.ld0, 16)
+        g.sync.dma_start(*loads[1][0]).then_inc(S.ld1, 16)
+        for buf, x in loads[2]:
+            g.scalar.dma_start(buf, x).then_inc(S.ld2, 16)
+        for c in range(3):
+            g.wait_ge(S["ld%d" % c], 16 * len(loads[c]))
+            trs = []
+            for e in range(8):
+                k = (pair + 1 + e) % 8
+                trs.append(RemoteDMATransfer(
+                    dst_ids=[dst_id(T.cores[2 * k + par] - 5 + HELPER[c])], dma_engine_mask=(1 << e) if e < 7 else ON,
+                    remote_sem=S["land%d" % c], src=bucket(c, k), dst=slot(c, pair)))
+            g.remote_dma_fused(trs, local_sem=S.sent)
+        g.sync.wait_ge(S.arr0, 64)
+        g.sync.dma_start(stores[0][0][1], stores[0][0][0]).then_inc(S.stored, 16)
+        g.scalar.wait_ge(S.arr1, 64)
+        g.scalar.dma_start(stores[1][0][1], stores[1][0][0]).then_inc(S.stored, 16)
+        g.sync.wait_ge(S.arr2, 64)
+        g.scalar.wait_ge(S.arr2, 64)
+        for i, (buf, y) in enumerate(stores[2]):
+            (g.sync, g.scalar)[i % 2].dma_start(y, buf).then_inc(S.stored, 16)
+        g.wait_ge(S.sent, 3 * 15)
+        for c in range(3):
+            g.wait_ge(S["arr%d" % c], 64)
+        g.wait_ge(S.stored, 16 * 7)
         return
 
-    k = pair
-    g.wait_ge(S.landed, 8 * 8)
-    mate = T.cores[rank ^ 1] - 5 + HELPER
-    rid, pid = topo.addr(mate, core)
-    g.remote_dma_fused([RemoteDMATransfer(
-        dst_ids=[DstId(rid=rid, pnc=pid)], dma_engine_mask=OFF, remote_sem=S.mate,
-        srcs=[piece(k, s) for s in range(8)], dsts=[piece(k, 8)], alu_op=1)], local_sem=S.sent)
-    g.wait_ge(S.mate, 8)
-    ids = []
-    for q in range(8):
-        rid, pid = topo.addr(T.cores[2 * q + par], core)
-        ids.append(DstId(rid=rid, pnc=pid))
-    g.remote_dma_fused([RemoteDMATransfer(
-        dst_ids=ids, dma_engine_mask=OFF, remote_sem=S.arrived,
-        srcs=[piece(k, s) for s in range(9)], dsts=[bucket(k) for q in range(8)], alu_op=1)], local_sem=S.sent)
-    g.wait_ge(S.sent, 16)
+    n = 0
+    for c in range(3):
+        if HELPER[c] != me:
+            continue
+        g.wait_ge(S["land%d" % c], 7 + 8)
+        g.remote_dma_fused([RemoteDMATransfer(
+            dst_ids=[dst_id(T.cores[rank ^ 1] - 5 + me)], dma_engine_mask=OFF, remote_sem=S["mate%d" % c],
+            srcs=[slot(c, s) for s in range(8)], dsts=[slot(c, 8)], alu_op=1)], local_sem=S.sent)
+        g.wait_ge(S["mate%d" % c], 8)
+        g.remote_dma_fused([RemoteDMATransfer(
+            dst_ids=[dst_id(T.cores[2 * q + par]) for q in range(8)], dma_engine_mask=OFF, remote_sem=S["arr%d" % c],
+            srcs=[slot(c, s) for s in range(9)], dsts=[bucket(c, pair) for q in range(8)], alu_op=1)], local_sem=S.sent)
+        n += 16
+    g.wait_ge(S.sent, n)

@@ -1,98 +1,88 @@
 from concourse.bass import DstId, RemoteDMATransfer
 
-WU, WV = 64, 42
-HELPER = (2, 3, 2)
+FOLD = (6, 2, 7)
+SPREAD = (0, 1, 3)
 OFF = 0x00FF
 ON = 0xFF00
 
 SCRATCH = {
-    "u": ("dram", [16, 128, WU], "float32"),
-    "v": ("dram", [9 * 128, WV], "float32"),
+    "u": ("dram", [16 * 128, 64], "float32"),
+    "v": ("dram", [8 * 128, 42], "float32"),
 }
-SEMAPHORES = ["ld0", "ld1", "ld2", "land0", "land1", "land2", "mate0", "mate1", "mate2", "arr0", "arr1", "arr2",
+SEMAPHORES = ["ld0", "ld1", "ld2", "land0", "land1", "land2", "part0", "part1", "part2", "arr0", "arr1", "arr2",
               "sent", "stored"]
 
 
 def places(T, pre):
     t1, t2, t3, t4 = T[pre + "1"], T[pre + "2"], T[pre + "3"], T[pre + "4"]
     return [
-        [(T.u[0:8], t3[0:64, :])],
-        [(T.u[8:16], t3[64:128, :])],
-        [(T.v[0:768, :], t1[0:126, :]),
-         (T.v[768:960, :], t4[0:126, :]),
-         (T.v[960:976, 0:32], t1[126:128, :]),
-         (T.v[976:980, 0:32], t4[126:128, :]),
-         (T.v[980:984, 0:32], t2[:, :])],
-    ]
-
-
-def padding(T):
-    return [
-        (T.v[960:984, 32:42], T.x1[0, 0:240]),
-        (T.v[984:1024, :], T.x3[0:2, 0:840]),
+        [(0, T.u[0:1024, :], t3[21:85, :])],
+        [(0, T.u[1024:1712, :], t3[85:128, :]),
+         (1, T.u[1712:1888, :], t1[84:128, :]),
+         (1, T.u[1888:2016, :], t4[:, :]),
+         (1, T.u[2016:2018, :], t2[:, :])],
+        [(0, T.v[0:512, :], t3[0:21, :]),
+         (1, T.v[512:1024, :], t1[0:84, :])],
     ]
 
 
 def rank_program(g, core, T, topo):
     me = core % 8
     rank = T.rank_of(core - me + 5)
-    if rank is None or (me != 5 and me not in HELPER):
+    if rank is None or me == 4:
         return
     pair, par = rank // 2, rank % 2
     S = T.sem
 
-    def slot(c, s):
-        return T.u[s] if c < 2 else T.v[128 * s:128 * (s + 1), :]
+    def block(c, i):
+        return T.u[128 * i:128 * (i + 1), :] if c < 2 else T.v[128 * i:128 * (i + 1), :]
 
     def bucket(c, k):
-        return T.u[8 * c + k] if c < 2 else T.v[128 * k:128 * (k + 1), :]
+        return block(c, 8 * c + k if c < 2 else k)
 
     def dst_id(d):
         rid, pid = topo.addr(d, core)
         return DstId(rid=rid, pnc=pid)
 
     if me == 5:
-        loads = places(T, "x")
-        loads[2] = loads[2] + padding(T)
-        stores = places(T, "y")
-        g.sync.dma_start(*loads[0][0]).then_inc(S.ld0, 16)
-        g.sync.dma_start(*loads[1][0]).then_inc(S.ld1, 16)
-        for buf, x in loads[2]:
-            g.scalar.dma_start(buf, x).then_inc(S.ld2, 16)
+        q = (g.sync, g.scalar)
+        loads, stores = places(T, "x"), places(T, "y")
+        loads[1].append((1, T.u[2018:2048, :], T.x4[0:30, :]))
+        for c in range(3):
+            for i, buf, x in loads[c]:
+                q[i].dma_start(buf, x).then_inc(S["ld%d" % c], 16)
         for c in range(3):
             g.wait_ge(S["ld%d" % c], 16 * len(loads[c]))
             trs = []
             for e in range(8):
                 k = (pair + 1 + e) % 8
                 trs.append(RemoteDMATransfer(
-                    dst_ids=[dst_id(T.cores[2 * k + par] - 5 + HELPER[c])], dma_engine_mask=(1 << e) if e < 7 else ON,
-                    remote_sem=S["land%d" % c], src=bucket(c, k), dst=slot(c, pair)))
+                    dst_ids=[dst_id(T.cores[2 * k + par] - 5 + FOLD[c])], dma_engine_mask=(1 << e) if e < 7 else ON,
+                    remote_sem=S["land%d" % c], src=bucket(c, k), dst=block(c, pair)))
             g.remote_dma_fused(trs, local_sem=S.sent)
-        g.sync.wait_ge(S.arr0, 64)
-        g.sync.dma_start(stores[0][0][1], stores[0][0][0]).then_inc(S.stored, 16)
-        g.scalar.wait_ge(S.arr1, 64)
-        g.scalar.dma_start(stores[1][0][1], stores[1][0][0]).then_inc(S.stored, 16)
-        g.sync.wait_ge(S.arr2, 64)
-        g.scalar.wait_ge(S.arr2, 64)
-        for i, (buf, y) in enumerate(stores[2]):
-            (g.sync, g.scalar)[i % 2].dma_start(y, buf).then_inc(S.stored, 16)
+        n = 0
+        for c in range(3):
+            for i in sorted(set([i for i, buf, y in stores[c]])):
+                q[i].wait_ge(S["arr%d" % c], 64)
+            for i, buf, y in stores[c]:
+                q[i].dma_start(y, buf).then_inc(S.stored, 16)
+                n += 16
         g.wait_ge(S.sent, 3 * 15)
         for c in range(3):
             g.wait_ge(S["arr%d" % c], 64)
-        g.wait_ge(S.stored, 16 * 7)
-        return
-
-    n = 0
-    for c in range(3):
-        if HELPER[c] != me:
-            continue
+        g.wait_ge(S.stored, n)
+    elif me in FOLD:
+        c = FOLD.index(me)
         g.wait_ge(S["land%d" % c], 7 + 8)
         g.remote_dma_fused([RemoteDMATransfer(
-            dst_ids=[dst_id(T.cores[rank ^ 1] - 5 + me)], dma_engine_mask=OFF, remote_sem=S["mate%d" % c],
-            srcs=[slot(c, s) for s in range(8)], dsts=[slot(c, 8)], alu_op=1)], local_sem=S.sent)
-        g.wait_ge(S["mate%d" % c], 8)
+            dst_ids=[dst_id(T.cores[r] - 5 + SPREAD[c]) for r in (rank, rank ^ 1)], dma_engine_mask=OFF,
+            remote_sem=S["part%d" % c], srcs=[block(c, s) for s in range(8)], dsts=[block(c, par), block(c, par)],
+            alu_op=1)], local_sem=S.sent)
+        g.wait_ge(S.sent, 8)
+    else:
+        c = SPREAD.index(me)
+        g.wait_ge(S["part%d" % c], 8 + 8)
         g.remote_dma_fused([RemoteDMATransfer(
-            dst_ids=[dst_id(T.cores[2 * q + par]) for q in range(8)], dma_engine_mask=OFF, remote_sem=S["arr%d" % c],
-            srcs=[slot(c, s) for s in range(9)], dsts=[bucket(c, pair) for q in range(8)], alu_op=1)], local_sem=S.sent)
-        n += 16
-    g.wait_ge(S.sent, n)
+            dst_ids=[dst_id(T.cores[2 * k + par]) for k in range(8)], dma_engine_mask=OFF, remote_sem=S["arr%d" % c],
+            srcs=[block(c, 0), block(c, 1)], dsts=[bucket(c, pair) for k in range(8)], alu_op=1)], local_sem=S.sent)
+        g.wait_ge(S.sent, 8)

@@ -9,8 +9,7 @@ SCRATCH = {
     "u": ("dram", [16 * 128, 64], "float32"),
     "v": ("dram", [8 * 128, 42], "float32"),
 }
-SEMAPHORES = ["ld0", "ld1", "ld2", "land0", "land1", "land2", "part0", "part1", "part2", "arr0", "arr1", "arr2",
-              "sent", "stored"]
+SEMAPHORES = ["ld0", "ld1", "ld2", "land", "part", "arr0", "arr1", "arr2", "sent", "stored"]
 
 
 def places(T, pre):
@@ -58,7 +57,7 @@ def rank_program(g, core, T, topo):
                 k = (pair + 1 + e) % 8
                 trs.append(RemoteDMATransfer(
                     dst_ids=[dst_id(T.cores[2 * k + par] - 5 + FOLD[c])], dma_engine_mask=(1 << e) if e < 7 else ON,
-                    remote_sem=S["land%d" % c], src=bucket(c, k), dst=block(c, pair)))
+                    remote_sem=S.land, src=bucket(c, k), dst=block(c, pair)))
             g.remote_dma_fused(trs, local_sem=S.sent)
         n = 0
         for c in range(3):
@@ -73,15 +72,15 @@ def rank_program(g, core, T, topo):
         g.wait_ge(S.stored, n)
     elif me in FOLD:
         c = FOLD.index(me)
-        g.wait_ge(S["land%d" % c], 7 + 8)
+        g.wait_ge(S.land, 7 + 8)
         g.remote_dma_fused([RemoteDMATransfer(
             dst_ids=[dst_id(T.cores[r] - 5 + SPREAD[c]) for r in (rank, rank ^ 1)], dma_engine_mask=OFF,
-            remote_sem=S["part%d" % c], srcs=[block(c, s) for s in range(8)], dsts=[block(c, par), block(c, par)],
+            remote_sem=S.part, srcs=[block(c, s) for s in range(8)], dsts=[block(c, par), block(c, par)],
             alu_op=1)], local_sem=S.sent)
         g.wait_ge(S.sent, 8)
     else:
         c = SPREAD.index(me)
-        g.wait_ge(S["part%d" % c], 8 + 8)
+        g.wait_ge(S.part, 8 + 8)
         g.remote_dma_fused([RemoteDMATransfer(
             dst_ids=[dst_id(T.cores[2 * k + par]) for k in range(8)], dma_engine_mask=OFF, remote_sem=S["arr%d" % c],
             srcs=[block(c, 0), block(c, 1)], dsts=[bucket(c, pair) for k in range(8)], alu_op=1)], local_sem=S.sent)

from concourse.bass import DstId, RemoteDMATransfer

FOLD = (6, 2, 7)
SPREAD = (0, 1, 3)
OFF = 0x00FF
ON = 0xFF00

SCRATCH = {
    "u": ("dram", [16 * 128, 64], "float32"),
    "v": ("dram", [8 * 128, 42], "float32"),
}
SEMAPHORES = ["ld0", "ld1", "ld2", "land", "part", "arr0", "arr1", "arr2", "sent", "stored"]


def places(T, pre):
    t1, t2, t3, t4 = T[pre + "1"], T[pre + "2"], T[pre + "3"], T[pre + "4"]
    return [
        [(0, T.u[0:1024, :], t3[21:85, :])],
        [(0, T.u[1024:1712, :], t3[85:128, :]),
         (1, T.u[1712:1888, :], t1[84:128, :]),
         (1, T.u[1888:2016, :], t4[:, :]),
         (1, T.u[2016:2018, :], t2[:, :])],
        [(0, T.v[0:512, :], t3[0:21, :]),
         (1, T.v[512:1024, :], t1[0:84, :])],
    ]


def rank_program(g, core, T, topo):
    me = core % 8
    rank = T.rank_of(core - me + 5)
    if rank is None or me == 4:
        return
    pair, par = rank // 2, rank % 2
    S = T.sem

    def block(c, i):
        return T.u[128 * i:128 * (i + 1), :] if c < 2 else T.v[128 * i:128 * (i + 1), :]

    def bucket(c, k):
        return block(c, 8 * c + k if c < 2 else k)

    def dst_id(d):
        rid, pid = topo.addr(d, core)
        return DstId(rid=rid, pnc=pid)

    if me == 5:
        q = (g.sync, g.scalar)
        loads, stores = places(T, "x"), places(T, "y")
        loads[1].append((1, T.u[2018:2048, :], T.x4[0:30, :]))
        for c in range(3):
            for i, buf, x in loads[c]:
                q[i].dma_start(buf, x).then_inc(S["ld%d" % c], 16)
        for c in range(3):
            g.wait_ge(S["ld%d" % c], 16 * len(loads[c]))
            trs = []
            for e in range(8):
                k = (pair + 1 + e) % 8
                trs.append(RemoteDMATransfer(
                    dst_ids=[dst_id(T.cores[2 * k + par] - 5 + FOLD[c])], dma_engine_mask=(1 << e) if e < 7 else ON,
                    remote_sem=S.land, src=bucket(c, k), dst=block(c, pair)))
            g.remote_dma_fused(trs, local_sem=S.sent)
        n = 0
        for c in range(3):
            for i in sorted(set([i for i, buf, y in stores[c]])):
                q[i].wait_ge(S["arr%d" % c], 64)
            for i, buf, y in stores[c]:
                q[i].dma_start(y, buf).then_inc(S.stored, 16)
                n += 16
        g.wait_ge(S.sent, 3 * 15)
        for c in range(3):
            g.wait_ge(S["arr%d" % c], 64)
        g.wait_ge(S.stored, n)
    elif me in FOLD:
        c = FOLD.index(me)
        g.wait_ge(S.land, 7 + 8)
        g.remote_dma_fused([RemoteDMATransfer(
            dst_ids=[dst_id(T.cores[r] - 5 + SPREAD[c]) for r in (rank, rank ^ 1)], dma_engine_mask=OFF,
            remote_sem=S.part, srcs=[block(c, s) for s in range(8)], dsts=[block(c, par), block(c, par)],
            alu_op=1)], local_sem=S.sent)
        g.wait_ge(S.sent, 8)
    else:
        c = SPREAD.index(me)
        g.wait_ge(S.part, 8 + 8)
        g.remote_dma_fused([RemoteDMATransfer(
            dst_ids=[dst_id(T.cores[2 * k + par]) for k in range(8)], dma_engine_mask=OFF, remote_sem=S["arr%d" % c],
            srcs=[block(c, 0), block(c, 1)], dsts=[bucket(c, pair) for k in range(8)], alu_op=1)], local_sem=S.sent)
        g.wait_ge(S.sent, 8)
